import numpy as np
import ml_dtypes


def mxq(x, axis, fmt="e4m3"):
    dtype, down = {"e4m3": (ml_dtypes.float8_e4m3fn, 7), "e5m2": (ml_dtypes.float8_e5m2, 14)}[fmt]
    v = np.moveaxis(np.asarray(x, np.float32).astype(ml_dtypes.bfloat16).astype(np.float64), axis, -1)
    blocks = v.reshape(v.shape[:-1] + (-1, 32))
    amax = np.abs(blocks).max(-1, keepdims=True)
    byte = np.maximum(np.where(amax > 0, np.frexp(amax)[1] - 1 + 127, 0) - down, 1)
    scale = np.exp2(byte - 127.0)
    codes = (blocks / scale).astype(np.float32).astype(dtype).astype(np.float64)
    return np.moveaxis((codes * scale).reshape(v.shape), -1, axis)


WIDE = False


def mx_kscale(k):
    if not WIDE:
        return np.ones(k)
    levels = np.array([10, -10, 5, -5, 0])
    if k % 512:
        return np.exp2(np.random.permutation(np.resize(levels, k // 32))).repeat(32)
    a = np.empty((k // 512, 16))
    for p in range(k // 512):
        a[p, :8] = np.random.permutation(np.resize(levels, 8))
        for g in range(8):
            far = levels[np.abs(levels - a[p, g]) >= 10]
            a[p, g + 8] = far[np.random.randint(len(far))]
    return np.exp2(a.ravel()).repeat(32)


def f64(x):
    return np.asarray(x).astype(np.float64)


def striped(idx):
    return np.tile(np.asarray(idx).reshape(-1, 16).T, (8, 1)).astype(np.uint16)


def unstriped(offs):
    return offs[:16].T.reshape(-1).astype(np.int64)


B, N, C, D, NQ = 1, 256, 4096, 1024, 256


def eight(codes):
    return np.concatenate([codes[h].reshape(-1, 16).T for h in range(8)]).astype(np.uint16)


def uneight(offs):
    return np.stack([offs[16 * h:16 * h + 16].T.reshape(-1) for h in range(8)]).astype(np.int64)


def setup_inputs():
    n = np.random.standard_normal
    s = mx_kscale(D)[:, None]
    grid = lambda x: np.round(x * 32) / 32
    return {
        "qT": (n((B, D, NQ)) * s / np.sqrt(D)).astype(np.float32),
        "cb": (grid(n((D, C))) / s).astype(np.float32),
        "norm": np.tile(np.random.randint(32, 129, N) / 64.0, (128, 1)).astype(np.float32),
        "offs": eight(np.random.randint(0, C, (8, N))),
        "offs2": eight(np.random.randint(0, C, (8, N))),
    }


def reference(qT, cb, norm, offs, offs2):
    k = []
    for part, offs_ in enumerate((offs, offs2,)):
        codes = uneight(offs_)
        k += [f64(cb)[512 * part + 64 * h:512 * part + 64 * h + 64][:, codes[h]] for h in range(8)]
    k = np.concatenate(k) * f64(norm)[:1]
    a = mxq(f64(qT), 1, "e4m3").transpose(0, 2, 1) @ mxq(k, 0, "e4m3")
    return a

@@ -1,0 +1,102 @@
+import concourse.mybir as mybir
+
+FLOPS = 2 * 256 * 256 * 1024
+
+F32 = mybir.dt.float32
+BF16 = mybir.dt.bfloat16
+U32 = mybir.dt.uint32
+U16 = mybir.dt.uint16
+U8 = mybir.dt.uint8
+FP8X4 = mybir.dt.float8_e4m3fn_x4
+MULT = mybir.AluOpType.mult
+
+P = 128
+PARTS = 2
+ROWS = 4
+CODEWORDS = 4096
+NQ = 256
+N = 256
+HALF = 128
+M_TILE = 128
+
+
+def tile_attend_pq_att_kernel(tc, qT, cb, norm, offs, offs2, out):
+    nc = tc.nc
+    rows = cb.rearrange("(g p t) c -> g t p c", g=PARTS, p=P, t=ROWS)
+    q_rows = qT[0].rearrange("(g p t) q -> g p t q", g=PARTS, t=ROWS)
+    halves = [slice(h * HALF, (h + 1) * HALF) for h in range(N // HALF)]
+    m_tiles = [slice(m * M_TILE, (m + 1) * M_TILE) for m in range(NQ // M_TILE)]
+
+    with (
+        tc.tile_pool(name="keep", bufs=1) as keep,
+        tc.psum_pool(name="psum", bufs=1) as psum,
+    ):
+        offsets = keep.tile([P, N // 16], U16, name="offsets")
+        offsets2 = keep.tile([P, N // 16], U16, name="offsets2")
+        scale = keep.tile([P, N], F32, name="scale")
+        q_raw = [keep.tile([P, ROWS, NQ], F32, name=f"q_raw_{g}") for g in range(PARTS)]
+        books = [
+            [keep.tile([P, CODEWORDS], F32, name=f"book_{g}_{t}") for t in range(ROWS)]
+            for g in range(PARTS)
+        ]
+
+        nc.sync.dma_start(books[0][0][:], rows[0, 0])
+        nc.sync.dma_start(offsets[:], offs)
+        nc.sync.dma_start(offsets2[:], offs2)
+        nc.scalar.dma_start(scale[:], norm)
+        for g in range(PARTS):
+            for t in range(ROWS):
+                if (g, t) > (0, 0):
+                    nc.sync.dma_start(books[g][t][:], rows[g, t])
+        for g in range(PARTS):
+            nc.sync.dma_start(q_raw[g][:], q_rows[g])
+
+        k_codes = [keep.tile([P, N], U32, name=f"k_codes_{g}", align_bytes=64) for g in range(PARTS)]
+        k_scales = [keep.tile([P, N], U8, name=f"k_scales_{g}", align_bytes=64) for g in range(PARTS)]
+        for g, lists in enumerate((offsets, offsets2)):
+            picked = [keep.tile([P, ROWS, HALF], F32, name=f"picked_{g}_{h}") for h in range(len(halves))]
+            k_bf = [keep.tile([P, HALF, ROWS], BF16, name=f"k_bf_{g}_{h}", align_bytes=64) for h in range(len(halves))]
+            for t in range(ROWS):
+                for h, cols in enumerate(halves):
+                    codes = lists[:, h * HALF // 16 : (h + 1) * HALF // 16]
+                    nc.vector.tensor_tensor(
+                        picked[h][:, t, :], books[g][t][:].indirect(codes), scale[:, cols], MULT
+                    )
+            nc.scalar.copy(k_bf[0][:], picked[0][:].rearrange("p t n -> p n t"))
+            nc.vector.tensor_copy(k_bf[1][:], picked[1][:].rearrange("p t n -> p n t"))
+            for h, cols in enumerate(halves):
+                nc.vector.quantize_mx(
+                    out=k_codes[g][:, cols].bitcast(FP8X4),
+                    scales=k_scales[g][:, cols],
+                    in_=k_bf[h][:].rearrange("p n t -> p (n t)"),
+                )
+
+        sums = [psum.tile([M_TILE, N], F32, name=f"sums_{m}") for m in range(len(m_tiles))]
+        for g in range(PARTS):
+            q_bf = [keep.tile([P, M_TILE, ROWS], BF16, name=f"q_bf_{g}_{m}", align_bytes=64) for m in range(len(m_tiles))]
+            q_codes = [keep.tile([P, M_TILE], U32, name=f"q_codes_{g}_{m}", align_bytes=64) for m in range(len(m_tiles))]
+            q_scales = [keep.tile([P, M_TILE], U8, name=f"q_scales_{g}_{m}", align_bytes=64) for m in range(len(m_tiles))]
+            nc.scalar.copy(q_bf[0][:], q_raw[g][:, :, m_tiles[0]].rearrange("p t q -> p q t"))
+            nc.vector.tensor_copy(q_bf[1][:], q_raw[g][:, :, m_tiles[1]].rearrange("p t q -> p q t"))
+            for m in reversed(range(len(m_tiles))):
+                nc.vector.quantize_mx(
+                    out=q_codes[m][:].bitcast(FP8X4),
+                    scales=q_scales[m][:],
+                    in_=q_bf[m][:].rearrange("p q t -> p (q t)"),
+                )
+            for m in reversed(range(len(m_tiles))):
+                nc.tensor.matmul_mx(
+                    out=sums[m][:],
+                    lhsT=q_codes[m][:].bitcast(FP8X4),
+                    lhsT_scale=q_scales[m][:],
+                    rhs=k_codes[g][:].bitcast(FP8X4),
+                    rhs_scale=k_scales[g][:],
+                    start=(g == 0),
+                    stop=(g == PARTS - 1),
+                )
+
+        results = [keep.tile([M_TILE, N], F32, name=f"result_{m}") for m in range(len(m_tiles))]
+        nc.vector.tensor_copy(results[1][:], sums[1][:])
+        nc.sync.dma_start(out[0, m_tiles[1], :], results[1][:])
+        nc.scalar.copy(results[0][:], sums[0][:])
+        nc.scalar.dma_start(out[0, m_tiles[0], :], results[0][:])

@@ -20,6 +20,10 @@ HALF = 128
 M_TILE = 128
 
 
+def weave(copy, dst, src):
+    copy(dst.rearrange("p (c i) t -> p c t i", i=4), src.rearrange("p t (c i) -> p c t i", i=4))
+
+
 def tile_attend_pq_att_kernel(tc, qT, cb, norm, offs, offs2, out):
     nc = tc.nc
     rows = cb.rearrange("(g p t) c -> g t p c", g=PARTS, p=P, t=ROWS)
@@ -33,6 +37,9 @@ def tile_attend_pq_att_kernel(tc, qT, cb, norm, offs, offs2, out):
     ):
         offsets = keep.tile([P, N // 16], U16, name="offsets")
         offsets2 = keep.tile([P, N // 16], U16, name="offsets2")
+        norm_part = keep.tile([P, 8], F32, name="norm_part")
+        norm_spread = keep.tile([P, 8, 32], F32, name="norm_spread", align_bytes=64)
+        norm_turned = keep.tile([P, N], F32, name="norm_turned", align_bytes=64)
         scale = keep.tile([P, N], F32, name="scale")
         q_raw = [keep.tile([P, ROWS, NQ], F32, name=f"q_raw_{g}") for g in range(PARTS)]
         books = [
@@ -43,7 +50,7 @@ def tile_attend_pq_att_kernel(tc, qT, cb, norm, offs, offs2, out):
         nc.sync.dma_start(books[0][0][:], rows[0, 0])
         nc.sync.dma_start(offsets[:], offs)
         nc.sync.dma_start(offsets2[:], offs2)
-        nc.scalar.dma_start(scale[:], norm)
+        nc.scalar.dma_start(norm_part[:], norm[0:4, :].rearrange("r (i e) -> (r i) e", e=8))
         for g in range(PARTS):
             for t in range(ROWS):
                 if (g, t) > (0, 0):
@@ -51,52 +58,74 @@ def tile_attend_pq_att_kernel(tc, qT, cb, norm, offs, offs2, out):
         for g in range(PARTS):
             nc.sync.dma_start(q_raw[g][:], q_rows[g])
 
+        nc.vector.tensor_copy(norm_spread[:], norm_part[:].unsqueeze(2).to_broadcast([P, 8, 32]))
+        nc.vector.transpose(norm_turned[:], norm_spread[:].rearrange("p e j -> p (e j)"))
+        nc.vector.tensor_copy(
+            scale[:].rearrange("p (i e) -> p i e", e=8), norm_turned[:].rearrange("p (e i) -> p i e", e=8)
+        )
+
+        picked = [
+            [keep.tile([P, ROWS, HALF], F32, name=f"picked_{g}_{h}") for h in range(len(halves))]
+            for g in range(PARTS)
+        ]
+        k_bf = [keep.tile([P, N, ROWS], BF16, name=f"k_bf_{g}", align_bytes=64) for g in range(PARTS)]
         k_codes = [keep.tile([P, N], U32, name=f"k_codes_{g}", align_bytes=64) for g in range(PARTS)]
         k_scales = [keep.tile([P, N], U8, name=f"k_scales_{g}", align_bytes=64) for g in range(PARTS)]
+        q_bf_first = keep.tile([P, M_TILE, ROWS], BF16, name="q_bf_first", align_bytes=64)
+        q_bf = [
+            [keep.tile([P, M_TILE, ROWS], BF16, name=f"q_bf_second_{g}", align_bytes=64), q_bf_first]
+            for g in range(PARTS)
+        ]
+        q_codes = [keep.tile([P, NQ], U32, name=f"q_codes_{g}", align_bytes=64) for g in range(PARTS)]
+        q_scales = [keep.tile([P, NQ], U8, name=f"q_scales_{g}", align_bytes=64) for g in range(PARTS)]
+        sums = [psum.tile([M_TILE, N], F32, name=f"sums_{m}") for m in range(len(m_tiles))]
+
+        def quantize(codes, scales, cols, values):
+            nc.vector.quantize_mx(
+                out=codes[:, cols].bitcast(FP8X4),
+                scales=scales[:, cols],
+                in_=values.rearrange("p c t -> p (c t)"),
+            )
+
+        def multiply(g, m):
+            nc.tensor.matmul_mx(
+                out=sums[m][:],
+                lhsT=q_codes[g][:, m_tiles[m]].bitcast(FP8X4),
+                lhsT_scale=q_scales[g][:, m_tiles[m]],
+                rhs=k_codes[g][:].bitcast(FP8X4),
+                rhs_scale=k_scales[g][:],
+                start=(g == 0),
+                stop=(g == PARTS - 1),
+            )
+
+        last = ROWS - 1
         for g, lists in enumerate((offsets, offsets2)):
-            picked = [keep.tile([P, ROWS, HALF], F32, name=f"picked_{g}_{h}") for h in range(len(halves))]
-            k_bf = [keep.tile([P, HALF, ROWS], BF16, name=f"k_bf_{g}_{h}", align_bytes=64) for h in range(len(halves))]
             for t in range(ROWS):
                 for h, cols in enumerate(halves):
                     codes = lists[:, h * HALF // 16 : (h + 1) * HALF // 16]
                     nc.vector.tensor_tensor(
-                        picked[h][:, t, :], books[g][t][:].indirect(codes), scale[:, cols], MULT
+                        picked[g][h][:, t, :], books[g][t][:].indirect(codes), scale[:, cols], MULT
                     )
-            nc.scalar.copy(k_bf[0][:], picked[0][:].rearrange("p t n -> p n t"))
-            nc.vector.tensor_copy(k_bf[1][:], picked[1][:].rearrange("p t n -> p n t"))
+                if t == last - 1:
+                    for h, cols in enumerate(halves):
+                        weave(nc.vector.tensor_copy, k_bf[g][:, cols, :last], picked[g][h][:, :last, :])
             for h, cols in enumerate(halves):
-                nc.vector.quantize_mx(
-                    out=k_codes[g][:, cols].bitcast(FP8X4),
-                    scales=k_scales[g][:, cols],
-                    in_=k_bf[h][:].rearrange("p n t -> p (n t)"),
-                )
+                nc.vector.tensor_copy(k_bf[g][:, cols, last], picked[g][h][:, last, :])
+            if g == 0:
+                quantize(k_codes[g], k_scales[g], slice(0, N), k_bf[g][:])
 
-        sums = [psum.tile([M_TILE, N], F32, name=f"sums_{m}") for m in range(len(m_tiles))]
         for g in range(PARTS):
-            q_bf = [keep.tile([P, M_TILE, ROWS], BF16, name=f"q_bf_{g}_{m}", align_bytes=64) for m in range(len(m_tiles))]
-            q_codes = [keep.tile([P, M_TILE], U32, name=f"q_codes_{g}_{m}", align_bytes=64) for m in range(len(m_tiles))]
-            q_scales = [keep.tile([P, M_TILE], U8, name=f"q_scales_{g}_{m}", align_bytes=64) for m in range(len(m_tiles))]
-            nc.scalar.copy(q_bf[0][:], q_raw[g][:, :, m_tiles[0]].rearrange("p t q -> p q t"))
-            nc.vector.tensor_copy(q_bf[1][:], q_raw[g][:, :, m_tiles[1]].rearrange("p t q -> p q t"))
-            for m in reversed(range(len(m_tiles))):
-                nc.vector.quantize_mx(
-                    out=q_codes[m][:].bitcast(FP8X4),
-                    scales=q_scales[m][:],
-                    in_=q_bf[m][:].rearrange("p q t -> p (q t)"),
-                )
-            for m in reversed(range(len(m_tiles))):
-                nc.tensor.matmul_mx(
-                    out=sums[m][:],
-                    lhsT=q_codes[m][:].bitcast(FP8X4),
-                    lhsT_scale=q_scales[m][:],
-                    rhs=k_codes[g][:].bitcast(FP8X4),
-                    rhs_scale=k_scales[g][:],
-                    start=(g == 0),
-                    stop=(g == PARTS - 1),
-                )
+            weave(nc.scalar.copy if g == 0 else nc.vector.tensor_copy, q_bf[g][1][:], q_raw[g][:, :, m_tiles[1]])
+            weave(nc.scalar.copy, q_bf[g][0][:], q_raw[g][:, :, m_tiles[0]])
+            if g == 0:
+                quantize(k_codes[1], k_scales[1], slice(0, N), k_bf[1][:])
+            for m in (1, 0):
+                quantize(q_codes[g], q_scales[g], m_tiles[m], q_bf[g][m][:])
+            for m in (1, 0):
+                multiply(g, m)
 
         results = [keep.tile([M_TILE, N], F32, name=f"result_{m}") for m in range(len(m_tiles))]
-        nc.vector.tensor_copy(results[1][:], sums[1][:])
-        nc.sync.dma_start(out[0, m_tiles[1], :], results[1][:])
-        nc.scalar.copy(results[0][:], sums[0][:])
-        nc.scalar.dma_start(out[0, m_tiles[0], :], results[0][:])
+        nc.scalar.copy(results[1][:], sums[1][:])
+        nc.scalar.dma_start(out[0, m_tiles[1], :], results[1][:])
+        nc.vector.tensor_copy(results[0][:], sums[0][:])
+        nc.sync.dma_start(out[0, m_tiles[0], :], results[0][:])

@@ -18,6 +18,7 @@ NQ = 256
 N = 256
 HALF = 128
 M_TILE = 128
+RUN_ROWS = (4, 2)
 
 
 def weave(copy, dst, src):
@@ -26,13 +27,14 @@ def weave(copy, dst, src):
 
 def tile_attend_pq_att_kernel(tc, qT, cb, norm, offs, offs2, out):
     nc = tc.nc
-    rows = cb.rearrange("(g p t) c -> g t p c", g=PARTS, p=P, t=ROWS)
+    rows = cb.rearrange("(g p t) c -> g p t c", g=PARTS, p=P, t=ROWS)
     q_rows = qT[0].rearrange("(g p t) q -> g p t q", g=PARTS, t=ROWS)
     halves = [slice(h * HALF, (h + 1) * HALF) for h in range(N // HALF)]
     m_tiles = [slice(m * M_TILE, (m + 1) * M_TILE) for m in range(NQ // M_TILE)]
 
     with (
         tc.tile_pool(name="keep", bufs=1) as keep,
+        tc.tile_pool(name="ring", bufs=2) as ring,
         tc.psum_pool(name="psum", bufs=1) as psum,
     ):
         offsets = keep.tile([P, N // 16], U16, name="offsets")
@@ -42,19 +44,18 @@ def tile_attend_pq_att_kernel(tc, qT, cb, norm, offs, offs2, out):
         norm_turned = keep.tile([P, N], F32, name="norm_turned", align_bytes=64)
         scale = keep.tile([P, N], F32, name="scale")
         q_raw = [keep.tile([P, ROWS, NQ], F32, name=f"q_raw_{g}") for g in range(PARTS)]
-        books = [
-            [keep.tile([P, CODEWORDS], F32, name=f"book_{g}_{t}") for t in range(ROWS)]
-            for g in range(PARTS)
-        ]
+        runs = [keep.tile([P, n, CODEWORDS], F32, name=f"run_{g}") for g, n in enumerate(RUN_ROWS)]
+        books = {
+            (PARTS - 1, t): keep.tile([P, CODEWORDS], F32, name=f"book_{t}") for t in range(RUN_ROWS[-1], ROWS)
+        }
 
-        nc.sync.dma_start(books[0][0][:], rows[0, 0])
+        nc.sync.dma_start(runs[0][:], rows[0])
         nc.sync.dma_start(offsets[:], offs)
         nc.sync.dma_start(offsets2[:], offs2)
         nc.scalar.dma_start(norm_part[:], norm[0:4, :].rearrange("r (i e) -> (r i) e", e=8))
-        for g in range(PARTS):
-            for t in range(ROWS):
-                if (g, t) > (0, 0):
-                    nc.sync.dma_start(books[g][t][:], rows[g, t])
+        nc.sync.dma_start(runs[1][:], rows[1, :, : RUN_ROWS[1], :])
+        for (g, t), book in books.items():
+            nc.sync.dma_start(book[:], rows[g, :, t, :])
         for g in range(PARTS):
             nc.sync.dma_start(q_raw[g][:], q_rows[g])
 
@@ -101,10 +102,16 @@ def tile_attend_pq_att_kernel(tc, qT, cb, norm, offs, offs2, out):
         last = ROWS - 1
         for g, lists in enumerate((offsets, offsets2)):
             for t in range(ROWS):
+                if t < RUN_ROWS[g]:
+                    by_scalar = t % 2 == 1
+                    book = ring.tile([P, CODEWORDS], F32, name="by_scalar" if by_scalar else "by_vector")
+                    (nc.scalar.copy if by_scalar else nc.vector.tensor_copy)(book[:], runs[g][:, t, :])
+                else:
+                    book = books[g, t]
                 for h, cols in enumerate(halves):
                     codes = lists[:, h * HALF // 16 : (h + 1) * HALF // 16]
                     nc.vector.tensor_tensor(
-                        picked[g][h][:, t, :], books[g][t][:].indirect(codes), scale[:, cols], MULT
+                        picked[g][h][:, t, :], book[:].indirect(codes), scale[:, cols], MULT
                     )
                 if t == last - 1:
                     for h, cols in enumerate(halves):

@@ -43,7 +43,11 @@ def tile_attend_pq_att_kernel(tc, qT, cb, norm, offs, offs2, out):
         norm_spread = keep.tile([P, 8, 32], F32, name="norm_spread", align_bytes=64)
         norm_turned = keep.tile([P, N], F32, name="norm_turned", align_bytes=64)
         scale = keep.tile([P, N], F32, name="scale")
-        q_raw = [keep.tile([P, ROWS, NQ], F32, name=f"q_raw_{g}") for g in range(PARTS)]
+        q_space = keep.tile([P, ROWS * NQ + M_TILE], F32, name="q_space", align_bytes=64)
+        q_raw = [
+            q_space[:, : ROWS * NQ].rearrange("p (t q) -> p t q", t=ROWS),
+            keep.tile([P, ROWS, NQ], F32, name="q_raw_1")[:],
+        ]
         runs = [keep.tile([P, n, CODEWORDS], F32, name=f"run_{g}") for g, n in enumerate(RUN_ROWS)]
         books = {
             (PARTS - 1, t): keep.tile([P, CODEWORDS], F32, name=f"book_{t}") for t in range(RUN_ROWS[-1], ROWS)
@@ -57,7 +61,7 @@ def tile_attend_pq_att_kernel(tc, qT, cb, norm, offs, offs2, out):
         for (g, t), book in books.items():
             nc.sync.dma_start(book[:], rows[g, :, t, :])
         for g in range(PARTS):
-            nc.sync.dma_start(q_raw[g][:], q_rows[g])
+            nc.sync.dma_start(q_raw[g], q_rows[g])
 
         nc.vector.tensor_copy(norm_spread[:], norm_part[:].unsqueeze(2).to_broadcast([P, 8, 32]))
         nc.vector.transpose(norm_turned[:], norm_spread[:].rearrange("p e j -> p (e j)"))
@@ -72,10 +76,12 @@ def tile_attend_pq_att_kernel(tc, qT, cb, norm, offs, offs2, out):
         k_bf = [keep.tile([P, N, ROWS], BF16, name=f"k_bf_{g}", align_bytes=64) for g in range(PARTS)]
         k_codes = [keep.tile([P, N], U32, name=f"k_codes_{g}", align_bytes=64) for g in range(PARTS)]
         k_scales = [keep.tile([P, N], U8, name=f"k_scales_{g}", align_bytes=64) for g in range(PARTS)]
-        q_bf_first = keep.tile([P, M_TILE, ROWS], BF16, name="q_bf_first", align_bytes=64)
         q_bf = [
-            [keep.tile([P, M_TILE, ROWS], BF16, name=f"q_bf_second_{g}", align_bytes=64), q_bf_first]
-            for g in range(PARTS)
+            [keep.tile([P, M_TILE, ROWS], BF16, name=f"q_bf_0_{m}", align_bytes=64)[:] for m in range(len(m_tiles))],
+            [
+                keep.tile([P, M_TILE, ROWS], BF16, name="q_bf_1_0", align_bytes=64)[:],
+                q_space[:, ROWS * NQ - M_TILE :].bitcast(BF16).rearrange("p (q t) -> p q t", t=ROWS),
+            ],
         ]
         q_codes = [keep.tile([P, NQ], U32, name=f"q_codes_{g}", align_bytes=64) for g in range(PARTS)]
         q_scales = [keep.tile([P, NQ], U8, name=f"q_scales_{g}", align_bytes=64) for g in range(PARTS)]
@@ -122,12 +128,12 @@ def tile_attend_pq_att_kernel(tc, qT, cb, norm, offs, offs2, out):
                 quantize(k_codes[g], k_scales[g], slice(0, N), k_bf[g][:])
 
         for g in range(PARTS):
-            weave(nc.scalar.copy if g == 0 else nc.vector.tensor_copy, q_bf[g][1][:], q_raw[g][:, :, m_tiles[1]])
-            weave(nc.scalar.copy, q_bf[g][0][:], q_raw[g][:, :, m_tiles[0]])
+            weave(nc.scalar.copy if g == 0 else nc.vector.tensor_copy, q_bf[g][1], q_raw[g][:, :, m_tiles[1]])
+            weave(nc.scalar.copy, q_bf[g][0], q_raw[g][:, :, m_tiles[0]])
             if g == 0:
                 quantize(k_codes[1], k_scales[1], slice(0, N), k_bf[1][:])
             for m in (1, 0):
-                quantize(q_codes[g], q_scales[g], m_tiles[m], q_bf[g][m][:])
+                quantize(q_codes[g], q_scales[g], m_tiles[m], q_bf[g][m])
             for m in (1, 0):
                 multiply(g, m)
 

@@ -85,7 +85,11 @@ def tile_attend_pq_att_kernel(tc, qT, cb, norm, offs, offs2, out):
         ]
         q_codes = [keep.tile([P, NQ], U32, name=f"q_codes_{g}", align_bytes=64) for g in range(PARTS)]
         q_scales = [keep.tile([P, NQ], U8, name=f"q_scales_{g}", align_bytes=64) for g in range(PARTS)]
-        sums = [psum.tile([M_TILE, N], F32, name=f"sums_{m}") for m in range(len(m_tiles))]
+        pieces = [halves, halves]
+        sums = [
+            [psum.tile([M_TILE, cols.stop - cols.start], F32, name=f"sums_{m}_{i}") for i, cols in enumerate(pieces[m])]
+            for m in range(len(m_tiles))
+        ]
 
         def quantize(codes, scales, cols, values):
             nc.vector.quantize_mx(
@@ -95,15 +99,16 @@ def tile_attend_pq_att_kernel(tc, qT, cb, norm, offs, offs2, out):
             )
 
         def multiply(g, m):
-            nc.tensor.matmul_mx(
-                out=sums[m][:],
-                lhsT=q_codes[g][:, m_tiles[m]].bitcast(FP8X4),
-                lhsT_scale=q_scales[g][:, m_tiles[m]],
-                rhs=k_codes[g][:].bitcast(FP8X4),
-                rhs_scale=k_scales[g][:],
-                start=(g == 0),
-                stop=(g == PARTS - 1),
-            )
+            for bank, cols in zip(sums[m], pieces[m]):
+                nc.tensor.matmul_mx(
+                    out=bank[:],
+                    lhsT=q_codes[g][:, m_tiles[m]].bitcast(FP8X4),
+                    lhsT_scale=q_scales[g][:, m_tiles[m]],
+                    rhs=k_codes[g][:, cols].bitcast(FP8X4),
+                    rhs_scale=k_scales[g][:, cols],
+                    start=(g == 0),
+                    stop=(g == PARTS - 1),
+                )
 
         last = ROWS - 1
         for g, lists in enumerate((offsets, offsets2)):
@@ -138,7 +143,9 @@ def tile_attend_pq_att_kernel(tc, qT, cb, norm, offs, offs2, out):
                 multiply(g, m)
 
         results = [keep.tile([M_TILE, N], F32, name=f"result_{m}") for m in range(len(m_tiles))]
-        nc.scalar.copy(results[1][:], sums[1][:])
-        nc.scalar.dma_start(out[0, m_tiles[1], :], results[1][:])
-        nc.vector.tensor_copy(results[0][:], sums[0][:])
+        for bank, cols in zip(sums[1], pieces[1]):
+            nc.scalar.copy(results[1][:, cols], bank[:])
+        nc.sync.dma_start(out[0, m_tiles[1], :], results[1][:])
+        for bank, cols in zip(sums[0], pieces[0]):
+            nc.vector.tensor_copy(results[0][:, cols], bank[:])
         nc.sync.dma_start(out[0, m_tiles[0], :], results[0][:])

@@ -37,20 +37,20 @@ def tile_attend_pq_att_kernel(tc, qT, cb, norm, offs, offs2, out):
         tc.tile_pool(name="ring", bufs=2) as ring,
         tc.psum_pool(name="psum", bufs=1) as psum,
     ):
-        offsets = keep.tile([P, N // 16], U16, name="offsets")
-        offsets2 = keep.tile([P, N // 16], U16, name="offsets2")
-        norm_part = keep.tile([P, 8], F32, name="norm_part")
+        offsets = keep.tile([P, N // 16], U16, name="offsets", align_bytes=256)
+        offsets2 = keep.tile([P, N // 16], U16, name="offsets2", align_bytes=256)
+        norm_part = keep.tile([P, 8], F32, name="norm_part", align_bytes=256)
         norm_spread = keep.tile([P, 8, 32], F32, name="norm_spread", align_bytes=64)
         norm_turned = keep.tile([P, N], F32, name="norm_turned", align_bytes=64)
         scale = keep.tile([P, N], F32, name="scale")
-        q_space = keep.tile([P, ROWS * NQ + M_TILE], F32, name="q_space", align_bytes=64)
+        q_space = keep.tile([P, ROWS * NQ + M_TILE], F32, name="q_space", align_bytes=256)
         q_raw = [
             q_space[:, : ROWS * NQ].rearrange("p (t q) -> p t q", t=ROWS),
-            keep.tile([P, ROWS, NQ], F32, name="q_raw_1")[:],
+            keep.tile([P, ROWS, NQ], F32, name="q_raw_1", align_bytes=256)[:],
         ]
-        runs = [keep.tile([P, n, CODEWORDS], F32, name=f"run_{g}") for g, n in enumerate(RUN_ROWS)]
+        runs = [keep.tile([P, n, CODEWORDS], F32, name=f"run_{g}", align_bytes=256) for g, n in enumerate(RUN_ROWS)]
         books = {
-            (PARTS - 1, t): keep.tile([P, CODEWORDS], F32, name=f"book_{t}") for t in range(RUN_ROWS[-1], ROWS)
+            (PARTS - 1, t): keep.tile([P, CODEWORDS], F32, name=f"book_{t}", align_bytes=256) for t in range(RUN_ROWS[-1], ROWS)
         }
 
         nc.sync.dma_start(runs[0][:], rows[0])
@@ -142,7 +142,7 @@ def tile_attend_pq_att_kernel(tc, qT, cb, norm, offs, offs2, out):
             for m in (1, 0):
                 multiply(g, m)
 
-        results = [keep.tile([M_TILE, N], F32, name=f"result_{m}") for m in range(len(m_tiles))]
+        results = [keep.tile([M_TILE, N], F32, name=f"result_{m}", align_bytes=256) for m in range(len(m_tiles))]
         for bank, cols in zip(sums[1], pieces[1]):
             nc.scalar.copy(results[1][:, cols], bank[:])
         nc.sync.dma_start(out[0, m_tiles[1], :], results[1][:])

@@ -46,7 +46,9 @@ def tile_attend_pq_att_kernel(tc, qT, cb, norm, offs, offs2, out):
         q_space = keep.tile([P, ROWS * NQ + M_TILE], F32, name="q_space", align_bytes=256)
         q_raw = [
             q_space[:, : ROWS * NQ].rearrange("p (t q) -> p t q", t=ROWS),
-            keep.tile([P, ROWS, NQ], F32, name="q_raw_1", align_bytes=256)[:],
+        ]
+        q_last = [
+            keep.tile([P, ROWS, M_TILE], F32, name=f"q_last_{m}", align_bytes=256) for m in range(len(m_tiles))
         ]
         runs = [keep.tile([P, n, CODEWORDS], F32, name=f"run_{g}", align_bytes=256) for g, n in enumerate(RUN_ROWS)]
         books = {
@@ -60,8 +62,10 @@ def tile_attend_pq_att_kernel(tc, qT, cb, norm, offs, offs2, out):
         nc.sync.dma_start(runs[1][:], rows[1, :, : RUN_ROWS[1], :])
         for (g, t), book in books.items():
             nc.sync.dma_start(book[:], rows[g, :, t, :])
-        for g in range(PARTS):
-            nc.sync.dma_start(q_raw[g], q_rows[g])
+        nc.sync.dma_start(q_raw[0], q_rows[0])
+        for m in (1, 0):
+            nc.sync.dma_start(q_last[m][:], q_rows[1][:, :, m_tiles[m]])
+        q_in = [[q_raw[0][:, :, cols] for cols in m_tiles], [tile[:] for tile in q_last]]
 
         nc.vector.tensor_copy(norm_spread[:], norm_part[:].unsqueeze(2).to_broadcast([P, 8, 32]))
         nc.vector.transpose(norm_turned[:], norm_spread[:].rearrange("p e j -> p (e j)"))
@@ -133,8 +137,8 @@ def tile_attend_pq_att_kernel(tc, qT, cb, norm, offs, offs2, out):
                 quantize(k_codes[g], k_scales[g], slice(0, N), k_bf[g][:])
 
         for g in range(PARTS):
-            weave(nc.scalar.copy if g == 0 else nc.vector.tensor_copy, q_bf[g][1], q_raw[g][:, :, m_tiles[1]])
-            weave(nc.scalar.copy, q_bf[g][0], q_raw[g][:, :, m_tiles[0]])
+            weave(nc.scalar.copy if g == 0 else nc.vector.tensor_copy, q_bf[g][1], q_in[g][1])
+            weave(nc.scalar.copy, q_bf[g][0], q_in[g][0])
             if g == 0:
                 quantize(k_codes[1], k_scales[1], slice(0, N), k_bf[1][:])
             for m in (1, 0):
@@ -146,6 +150,6 @@ def tile_attend_pq_att_kernel(tc, qT, cb, norm, offs, offs2, out):
         for bank, cols in zip(sums[1], pieces[1]):
             nc.scalar.copy(results[1][:, cols], bank[:])
         nc.sync.dma_start(out[0, m_tiles[1], :], results[1][:])
-        for bank, cols in zip(sums[0], pieces[0]):
-            nc.vector.tensor_copy(results[0][:, cols], bank[:])
+        for copy, bank, cols in zip((nc.vector.tensor_copy, nc.scalar.copy), sums[0], pieces[0]):
+            copy(results[0][:, cols], bank[:])
         nc.sync.dma_start(out[0, m_tiles[0], :], results[0][:])

@@ -43,13 +43,11 @@ def tile_attend_pq_att_kernel(tc, qT, cb, norm, offs, offs2, out):
         norm_spread = keep.tile([P, 8, 32], F32, name="norm_spread", align_bytes=64)
         norm_turned = keep.tile([P, N], F32, name="norm_turned", align_bytes=64)
         scale = keep.tile([P, N], F32, name="scale")
-        q_space = keep.tile([P, ROWS * NQ + M_TILE], F32, name="q_space", align_bytes=256)
-        q_raw = [
-            q_space[:, : ROWS * NQ].rearrange("p (t q) -> p t q", t=ROWS),
-        ]
-        q_last = [
-            keep.tile([P, ROWS, M_TILE], F32, name=f"q_last_{m}", align_bytes=256) for m in range(len(m_tiles))
-        ]
+        q_raw = {
+            (g, m): keep.tile([P, ROWS, M_TILE], F32, name=f"q_raw_{g}_{m}", align_bytes=256)
+            for g in range(PARTS)
+            for m in range(len(m_tiles))
+        }
         runs = [keep.tile([P, n, CODEWORDS], F32, name=f"run_{g}", align_bytes=256) for g, n in enumerate(RUN_ROWS)]
         books = {
             (PARTS - 1, t): keep.tile([P, CODEWORDS], F32, name=f"book_{t}", align_bytes=256) for t in range(RUN_ROWS[-1], ROWS)
@@ -62,10 +60,8 @@ def tile_attend_pq_att_kernel(tc, qT, cb, norm, offs, offs2, out):
         nc.sync.dma_start(runs[1][:], rows[1, :, : RUN_ROWS[1], :])
         for (g, t), book in books.items():
             nc.sync.dma_start(book[:], rows[g, :, t, :])
-        nc.sync.dma_start(q_raw[0], q_rows[0])
-        for m in (1, 0):
-            nc.sync.dma_start(q_last[m][:], q_rows[1][:, :, m_tiles[m]])
-        q_in = [[q_raw[0][:, :, cols] for cols in m_tiles], [tile[:] for tile in q_last]]
+        for g, m in ((0, 1), (1, 1), (0, 0), (1, 0)):
+            nc.sync.dma_start(q_raw[g, m][:], q_rows[g][:, :, m_tiles[m]])
 
         nc.vector.tensor_copy(norm_spread[:], norm_part[:].unsqueeze(2).to_broadcast([P, 8, 32]))
         nc.vector.transpose(norm_turned[:], norm_spread[:].rearrange("p e j -> p (e j)"))
@@ -79,14 +75,18 @@ def tile_attend_pq_att_kernel(tc, qT, cb, norm, offs, offs2, out):
         ]
         k_bf = [keep.tile([P, N, ROWS], BF16, name=f"k_bf_{g}", align_bytes=64) for g in range(PARTS)]
         k_codes = [keep.tile([P, N], U32, name=f"k_codes_{g}", align_bytes=64) for g in range(PARTS)]
-        k_scales = [keep.tile([P, N], U8, name=f"k_scales_{g}", align_bytes=64) for g in range(PARTS)]
-        q_bf = [
-            [keep.tile([P, M_TILE, ROWS], BF16, name=f"q_bf_0_{m}", align_bytes=64)[:] for m in range(len(m_tiles))],
-            [
-                keep.tile([P, M_TILE, ROWS], BF16, name="q_bf_1_0", align_bytes=64)[:],
-                q_space[:, ROWS * NQ - M_TILE :].bitcast(BF16).rearrange("p (q t) -> p q t", t=ROWS),
-            ],
+        k_scales = [
+            keep.tile([P, N], U8, name="k_scales_0", align_bytes=64),
+            keep.tile([P, N], U8, name="q_raw_0_1", align_bytes=256),
         ]
+        q_bf = {
+            key: keep.tile([P, M_TILE, ROWS], BF16, name=f"q_bf_{key[0]}_{key[1]}", align_bytes=64)[:]
+            for key in q_raw
+            if key != (1, 0)
+        }
+        q_bf[1, 0] = (
+            q_raw[1, 1][:, ROWS // 2 :, :].rearrange("p t q -> p (t q)").bitcast(BF16).rearrange("p (q t) -> p q t", t=ROWS)
+        )
         q_codes = [keep.tile([P, NQ], U32, name=f"q_codes_{g}", align_bytes=64) for g in range(PARTS)]
         q_scales = [keep.tile([P, NQ], U8, name=f"q_scales_{g}", align_bytes=64) for g in range(PARTS)]
         pieces = [halves, halves]
@@ -136,20 +136,25 @@ def tile_attend_pq_att_kernel(tc, qT, cb, norm, offs, offs2, out):
             if g == 0:
                 quantize(k_codes[g], k_scales[g], slice(0, N), k_bf[g][:])
 
+        def prepare(g, m, copy):
+            weave(copy, q_bf[g, m], q_raw[g, m][:])
+            quantize(q_codes[g], q_scales[g], m_tiles[m], q_bf[g, m])
+
+        prepare(0, 1, nc.scalar.copy)
+        multiply(0, 1)
+        quantize(k_codes[1], k_scales[1], slice(0, N), k_bf[1][:])
+        prepare(1, 1, nc.scalar.copy)
+        multiply(1, 1)
+        weave(nc.scalar.copy, q_bf[0, 0], q_raw[0, 0][:])
+        weave(nc.vector.tensor_copy, q_bf[1, 0], q_raw[1, 0][:])
         for g in range(PARTS):
-            weave(nc.scalar.copy if g == 0 else nc.vector.tensor_copy, q_bf[g][1], q_in[g][1])
-            weave(nc.scalar.copy, q_bf[g][0], q_in[g][0])
-            if g == 0:
-                quantize(k_codes[1], k_scales[1], slice(0, N), k_bf[1][:])
-            for m in (1, 0):
-                quantize(q_codes[g], q_scales[g], m_tiles[m], q_bf[g][m])
-            for m in (1, 0):
-                multiply(g, m)
+            quantize(q_codes[g], q_scales[g], m_tiles[0], q_bf[g, 0])
+            multiply(g, 0)
 
         results = [keep.tile([M_TILE, N], F32, name=f"result_{m}", align_bytes=256) for m in range(len(m_tiles))]
         for bank, cols in zip(sums[1], pieces[1]):
             nc.scalar.copy(results[1][:, cols], bank[:])
         nc.sync.dma_start(out[0, m_tiles[1], :], results[1][:])
-        for copy, bank, cols in zip((nc.vector.tensor_copy, nc.scalar.copy), sums[0], pieces[0]):
+        for copy, bank, cols in zip((nc.scalar.copy, nc.vector.tensor_copy), sums[0], pieces[0]):
             copy(results[0][:, cols], bank[:])
         nc.sync.dma_start(out[0, m_tiles[0], :], results[0][:])

@@ -18,6 +18,7 @@ NQ = 256
 N = 256
 HALF = 128
 M_TILE = 128
+SHARE = 64
 RUN_ROWS = (4, 2)
 
 
@@ -77,16 +78,9 @@ def tile_attend_pq_att_kernel(tc, qT, cb, norm, offs, offs2, out):
         k_codes = [keep.tile([P, N], U32, name=f"k_codes_{g}", align_bytes=64) for g in range(PARTS)]
         k_scales = [
             keep.tile([P, N], U8, name="k_scales_0", align_bytes=64),
-            keep.tile([P, N], U8, name="q_raw_0_1", align_bytes=256),
+            keep.tile([P, N], U8, name="q_raw_1_1", align_bytes=256),
         ]
-        q_bf = {
-            key: keep.tile([P, M_TILE, ROWS], BF16, name=f"q_bf_{key[0]}_{key[1]}", align_bytes=64)[:]
-            for key in q_raw
-            if key != (1, 0)
-        }
-        q_bf[1, 0] = (
-            q_raw[1, 1][:, ROWS // 2 :, :].rearrange("p t q -> p (t q)").bitcast(BF16).rearrange("p (q t) -> p q t", t=ROWS)
-        )
+        q_bf = {key: keep.tile([P, M_TILE, ROWS], BF16, name=f"q_bf_{key[0]}_{key[1]}", align_bytes=64)[:] for key in q_raw}
         q_codes = [keep.tile([P, NQ], U32, name=f"q_codes_{g}", align_bytes=64) for g in range(PARTS)]
         q_scales = [keep.tile([P, NQ], U8, name=f"q_scales_{g}", align_bytes=64) for g in range(PARTS)]
         pieces = [halves, halves]
@@ -136,22 +130,25 @@ def tile_attend_pq_att_kernel(tc, qT, cb, norm, offs, offs2, out):
             if g == 0:
                 quantize(k_codes[g], k_scales[g], slice(0, N), k_bf[g][:])
 
-        def prepare(g, m, copy):
-            weave(copy, q_bf[g, m], q_raw[g, m][:])
+        def finish(g, m):
             quantize(q_codes[g], q_scales[g], m_tiles[m], q_bf[g, m])
+            multiply(g, m)
 
-        prepare(0, 1, nc.scalar.copy)
-        multiply(0, 1)
+        weave(nc.scalar.copy, q_bf[0, 1], q_raw[0, 1][:])
+        weave(nc.vector.tensor_copy, q_bf[1, 1], q_raw[1, 1][:])
+        finish(0, 1)
         quantize(k_codes[1], k_scales[1], slice(0, N), k_bf[1][:])
-        prepare(1, 1, nc.scalar.copy)
-        multiply(1, 1)
+        finish(1, 1)
         weave(nc.scalar.copy, q_bf[0, 0], q_raw[0, 0][:])
-        weave(nc.vector.tensor_copy, q_bf[1, 0], q_raw[1, 0][:])
-        for g in range(PARTS):
-            quantize(q_codes[g], q_scales[g], m_tiles[0], q_bf[g, 0])
-            multiply(g, 0)
+        for copy, queries in ((nc.vector.tensor_copy, slice(0, SHARE)), (nc.scalar.copy, slice(SHARE, M_TILE))):
+            weave(copy, q_bf[1, 0][:, queries, :], q_raw[1, 0][:, :, queries])
+        finish(0, 0)
+        finish(1, 0)
 
-        results = [keep.tile([M_TILE, N], F32, name=f"result_{m}", align_bytes=256) for m in range(len(m_tiles))]
+        results = [
+            keep.tile([M_TILE, N], F32, name="result_0", align_bytes=256),
+            keep.tile([M_TILE, N], F32, name="q_raw_1_0", align_bytes=256),
+        ]
         for bank, cols in zip(sums[1], pieces[1]):
             nc.scalar.copy(results[1][:, cols], bank[:])
         nc.sync.dma_start(out[0, m_tiles[1], :], results[1][:])

@@ -152,6 +152,8 @@ def tile_attend_pq_att_kernel(tc, qT, cb, norm, offs, offs2, out):
         for bank, cols in zip(sums[1], pieces[1]):
             nc.scalar.copy(results[1][:, cols], bank[:])
         nc.sync.dma_start(out[0, m_tiles[1], :], results[1][:])
-        for copy, bank, cols in zip((nc.scalar.copy, nc.vector.tensor_copy), sums[0], pieces[0]):
+        for copy, queue, bank, cols in zip(
+            (nc.scalar.copy, nc.vector.tensor_copy), (nc.scalar, nc.sync), sums[0], pieces[0]
+        ):
             copy(results[0][:, cols], bank[:])
-        nc.sync.dma_start(out[0, m_tiles[0], :], results[0][:])
+            queue.dma_start(out[0, m_tiles[0], cols], results[0][:, cols])

@@ -18,7 +18,7 @@ NQ = 256
 N = 256
 HALF = 128
 M_TILE = 128
-SHARE = 64
+SHARE = 96
 RUN_ROWS = (4, 2)
 
 

@@ -18,12 +18,18 @@ NQ = 256
 N = 256
 HALF = 128
 M_TILE = 128
-SHARE = 96
+LIST_GROUP = 16
+BLOCK = 32
+NORM_RUN = N // BLOCK
+LINE = 4
+DMA_ALIGN = 256
+MX_ALIGN = 64
+SHARE = 80
 RUN_ROWS = (4, 2)
 
 
 def weave(copy, dst, src):
-    copy(dst.rearrange("p (c i) t -> p c t i", i=4), src.rearrange("p t (c i) -> p c t i", i=4))
+    copy(dst.rearrange("p (c i) t -> p c t i", i=LINE), src.rearrange("p t (c i) -> p c t i", i=LINE))
 
 
 def tile_attend_pq_att_kernel(tc, qT, cb, norm, offs, offs2, out):
@@ -38,54 +44,61 @@ def tile_attend_pq_att_kernel(tc, qT, cb, norm, offs, offs2, out):
         tc.tile_pool(name="ring", bufs=2) as ring,
         tc.psum_pool(name="psum", bufs=1) as psum,
     ):
-        offsets = keep.tile([P, N // 16], U16, name="offsets", align_bytes=256)
-        offsets2 = keep.tile([P, N // 16], U16, name="offsets2", align_bytes=256)
-        norm_part = keep.tile([P, 8], F32, name="norm_part", align_bytes=256)
-        norm_spread = keep.tile([P, 8, 32], F32, name="norm_spread", align_bytes=64)
-        norm_turned = keep.tile([P, N], F32, name="norm_turned", align_bytes=64)
-        scale = keep.tile([P, N], F32, name="scale")
+        offsets = keep.tile([P, N // LIST_GROUP], U16, name="offsets", align_bytes=DMA_ALIGN)
+        offsets2 = keep.tile([P, N // LIST_GROUP], U16, name="offsets2", align_bytes=DMA_ALIGN)
+        norm_part = keep.tile([P, NORM_RUN], F32, name="norm_part", align_bytes=DMA_ALIGN)
+        norm_spread = keep.tile([P, NORM_RUN, BLOCK], F32, name="norm_spread", align_bytes=MX_ALIGN)
+        norm_turned = keep.tile([P, N], F32, name="norm_turned", align_bytes=MX_ALIGN)
+        norm_row = keep.tile([P, N], F32, name="norm_row")
         q_raw = {
-            (g, m): keep.tile([P, ROWS, M_TILE], F32, name=f"q_raw_{g}_{m}", align_bytes=256)
+            (g, m): keep.tile([P, ROWS, M_TILE], F32, name=f"q_raw_{g}_{m}", align_bytes=DMA_ALIGN)
             for g in range(PARTS)
             for m in range(len(m_tiles))
         }
-        runs = [keep.tile([P, n, CODEWORDS], F32, name=f"run_{g}", align_bytes=256) for g, n in enumerate(RUN_ROWS)]
-        books = {
-            (PARTS - 1, t): keep.tile([P, CODEWORDS], F32, name=f"book_{t}", align_bytes=256) for t in range(RUN_ROWS[-1], ROWS)
+        runs = [
+            keep.tile([P, count, CODEWORDS], F32, name=f"run_{g}", align_bytes=DMA_ALIGN)
+            for g, count in enumerate(RUN_ROWS)
+        ]
+        loaded_windows = {
+            (PARTS - 1, t): keep.tile([P, CODEWORDS], F32, name=f"window_{t}", align_bytes=DMA_ALIGN)
+            for t in range(RUN_ROWS[-1], ROWS)
         }
 
         nc.sync.dma_start(runs[0][:], rows[0])
         nc.sync.dma_start(offsets[:], offs)
         nc.sync.dma_start(offsets2[:], offs2)
-        nc.scalar.dma_start(norm_part[:], norm[0:4, :].rearrange("r (i e) -> (r i) e", e=8))
+        nc.scalar.dma_start(norm_part[:], norm[0 : P // BLOCK, :].rearrange("r (i e) -> (r i) e", e=NORM_RUN))
         nc.sync.dma_start(runs[1][:], rows[1, :, : RUN_ROWS[1], :])
-        for (g, t), book in books.items():
-            nc.sync.dma_start(book[:], rows[g, :, t, :])
+        for (g, t), window in loaded_windows.items():
+            nc.sync.dma_start(window[:], rows[g, :, t, :])
         for g, m in ((0, 1), (1, 1), (0, 0), (1, 0)):
             nc.sync.dma_start(q_raw[g, m][:], q_rows[g][:, :, m_tiles[m]])
 
-        nc.vector.tensor_copy(norm_spread[:], norm_part[:].unsqueeze(2).to_broadcast([P, 8, 32]))
+        nc.vector.tensor_copy(norm_spread[:], norm_part[:].unsqueeze(2).to_broadcast([P, NORM_RUN, BLOCK]))
         nc.vector.transpose(norm_turned[:], norm_spread[:].rearrange("p e j -> p (e j)"))
         nc.vector.tensor_copy(
-            scale[:].rearrange("p (i e) -> p i e", e=8), norm_turned[:].rearrange("p (e i) -> p i e", e=8)
+            norm_row[:].rearrange("p (i e) -> p i e", e=NORM_RUN),
+            norm_turned[:].rearrange("p (e i) -> p i e", e=NORM_RUN),
         )
 
-        picked = [
-            [keep.tile([P, ROWS, HALF], F32, name=f"picked_{g}_{h}") for h in range(len(halves))]
+        k_f32 = [
+            [keep.tile([P, ROWS, HALF], F32, name=f"k_f32_{g}_{h}") for h in range(len(halves))]
             for g in range(PARTS)
         ]
-        k_bf = [keep.tile([P, N, ROWS], BF16, name=f"k_bf_{g}", align_bytes=64) for g in range(PARTS)]
-        k_codes = [keep.tile([P, N], U32, name=f"k_codes_{g}", align_bytes=64) for g in range(PARTS)]
+        k_bf = [keep.tile([P, N, ROWS], BF16, name=f"k_bf_{g}", align_bytes=MX_ALIGN) for g in range(PARTS)]
+        k_codes = [keep.tile([P, N], U32, name=f"k_codes_{g}", align_bytes=MX_ALIGN) for g in range(PARTS)]
         k_scales = [
-            keep.tile([P, N], U8, name="k_scales_0", align_bytes=64),
-            keep.tile([P, N], U8, name="q_raw_1_1", align_bytes=256),
+            keep.tile([P, N], U8, name="k_scales_0", align_bytes=MX_ALIGN),
+            keep.tile([P, N], U8, name="q_raw_1_1", align_bytes=DMA_ALIGN),
         ]
-        q_bf = {key: keep.tile([P, M_TILE, ROWS], BF16, name=f"q_bf_{key[0]}_{key[1]}", align_bytes=64)[:] for key in q_raw}
-        q_codes = [keep.tile([P, NQ], U32, name=f"q_codes_{g}", align_bytes=64) for g in range(PARTS)]
-        q_scales = [keep.tile([P, NQ], U8, name=f"q_scales_{g}", align_bytes=64) for g in range(PARTS)]
-        pieces = [halves, halves]
+        q_bf = {
+            (g, m): keep.tile([P, M_TILE, ROWS], BF16, name=f"q_bf_{g}_{m}", align_bytes=MX_ALIGN)[:]
+            for g, m in q_raw
+        }
+        q_codes = [keep.tile([P, NQ], U32, name=f"q_codes_{g}", align_bytes=MX_ALIGN) for g in range(PARTS)]
+        q_scales = [keep.tile([P, NQ], U8, name=f"q_scales_{g}", align_bytes=MX_ALIGN) for g in range(PARTS)]
         sums = [
-            [psum.tile([M_TILE, cols.stop - cols.start], F32, name=f"sums_{m}_{i}") for i, cols in enumerate(pieces[m])]
+            [psum.tile([M_TILE, HALF], F32, name=f"sums_{m}_{h}") for h in range(len(halves))]
             for m in range(len(m_tiles))
         ]
 
@@ -96,8 +109,9 @@ def tile_attend_pq_att_kernel(tc, qT, cb, norm, offs, offs2, out):
                 in_=values.rearrange("p c t -> p (c t)"),
             )
 
-        def multiply(g, m):
-            for bank, cols in zip(sums[m], pieces[m]):
+        def quantize_and_multiply(g, m):
+            quantize(q_codes[g], q_scales[g], m_tiles[m], q_bf[g, m])
+            for bank, cols in zip(sums[m], halves):
                 nc.tensor.matmul_mx(
                     out=bank[:],
                     lhsT=q_codes[g][:, m_tiles[m]].bitcast(FP8X4),
@@ -113,47 +127,43 @@ def tile_attend_pq_att_kernel(tc, qT, cb, norm, offs, offs2, out):
             for t in range(ROWS):
                 if t < RUN_ROWS[g]:
                     by_scalar = t % 2 == 1
-                    book = ring.tile([P, CODEWORDS], F32, name="by_scalar" if by_scalar else "by_vector")
-                    (nc.scalar.copy if by_scalar else nc.vector.tensor_copy)(book[:], runs[g][:, t, :])
+                    window = ring.tile([P, CODEWORDS], F32, name="by_scalar" if by_scalar else "by_vector")
+                    (nc.scalar.copy if by_scalar else nc.vector.tensor_copy)(window[:], runs[g][:, t, :])
                 else:
-                    book = books[g, t]
+                    window = loaded_windows[g, t]
                 for h, cols in enumerate(halves):
-                    codes = lists[:, h * HALF // 16 : (h + 1) * HALF // 16]
+                    entries = lists[:, h * HALF // LIST_GROUP : (h + 1) * HALF // LIST_GROUP]
                     nc.vector.tensor_tensor(
-                        picked[g][h][:, t, :], book[:].indirect(codes), scale[:, cols], MULT
+                        k_f32[g][h][:, t, :], window[:].indirect(entries), norm_row[:, cols], MULT
                     )
                 if t == last - 1:
                     for h, cols in enumerate(halves):
-                        weave(nc.vector.tensor_copy, k_bf[g][:, cols, :last], picked[g][h][:, :last, :])
+                        weave(nc.vector.tensor_copy, k_bf[g][:, cols, :last], k_f32[g][h][:, :last, :])
             for h, cols in enumerate(halves):
-                nc.vector.tensor_copy(k_bf[g][:, cols, last], picked[g][h][:, last, :])
+                nc.vector.tensor_copy(k_bf[g][:, cols, last], k_f32[g][h][:, last, :])
             if g == 0:
                 quantize(k_codes[g], k_scales[g], slice(0, N), k_bf[g][:])
 
-        def finish(g, m):
-            quantize(q_codes[g], q_scales[g], m_tiles[m], q_bf[g, m])
-            multiply(g, m)
-
         weave(nc.scalar.copy, q_bf[0, 1], q_raw[0, 1][:])
         weave(nc.vector.tensor_copy, q_bf[1, 1], q_raw[1, 1][:])
-        finish(0, 1)
+        quantize_and_multiply(0, 1)
         quantize(k_codes[1], k_scales[1], slice(0, N), k_bf[1][:])
-        finish(1, 1)
+        quantize_and_multiply(1, 1)
         weave(nc.scalar.copy, q_bf[0, 0], q_raw[0, 0][:])
         for copy, queries in ((nc.vector.tensor_copy, slice(0, SHARE)), (nc.scalar.copy, slice(SHARE, M_TILE))):
             weave(copy, q_bf[1, 0][:, queries, :], q_raw[1, 0][:, :, queries])
-        finish(0, 0)
-        finish(1, 0)
+        quantize_and_multiply(0, 0)
+        quantize_and_multiply(1, 0)
 
         results = [
-            keep.tile([M_TILE, N], F32, name="result_0", align_bytes=256),
-            keep.tile([M_TILE, N], F32, name="q_raw_1_0", align_bytes=256),
+            keep.tile([M_TILE, N], F32, name="result_0", align_bytes=DMA_ALIGN),
+            keep.tile([M_TILE, N], F32, name="q_raw_1_0", align_bytes=DMA_ALIGN),
         ]
-        for bank, cols in zip(sums[1], pieces[1]):
+        for bank, cols in zip(sums[1], halves):
             nc.scalar.copy(results[1][:, cols], bank[:])
         nc.sync.dma_start(out[0, m_tiles[1], :], results[1][:])
         for copy, queue, bank, cols in zip(
-            (nc.scalar.copy, nc.vector.tensor_copy), (nc.scalar, nc.sync), sums[0], pieces[0]
+            (nc.scalar.copy, nc.vector.tensor_copy), (nc.scalar, nc.sync), sums[0], halves
         ):
             copy(results[0][:, cols], bank[:])
             queue.dma_start(out[0, m_tiles[0], cols], results[0][:, cols])

@@ -50,11 +50,6 @@ def tile_attend_pq_att_kernel(tc, qT, cb, norm, offs, offs2, out):
         norm_spread = keep.tile([P, NORM_RUN, BLOCK], F32, name="norm_spread", align_bytes=MX_ALIGN)
         norm_turned = keep.tile([P, N], F32, name="norm_turned", align_bytes=MX_ALIGN)
         norm_row = keep.tile([P, N], F32, name="norm_row")
-        q_raw = {
-            (g, m): keep.tile([P, ROWS, M_TILE], F32, name=f"q_raw_{g}_{m}", align_bytes=DMA_ALIGN)
-            for g in range(PARTS)
-            for m in range(len(m_tiles))
-        }
         runs = [
             keep.tile([P, count, CODEWORDS], F32, name=f"run_{g}", align_bytes=DMA_ALIGN)
             for g, count in enumerate(RUN_ROWS)
@@ -62,6 +57,10 @@ def tile_attend_pq_att_kernel(tc, qT, cb, norm, offs, offs2, out):
         loaded_windows = {
             (PARTS - 1, t): keep.tile([P, CODEWORDS], F32, name=f"window_{t}", align_bytes=DMA_ALIGN)
             for t in range(RUN_ROWS[-1], ROWS)
+        }
+        q_raw = {
+            (g, m): keep.tile([P, ROWS, M_TILE], F32, name=f"q_raw_{g}_{m}", align_bytes=DMA_ALIGN)
+            for g, m in ((0, 0), (0, 1), (1, 1))
         }
 
         nc.sync.dma_start(runs[0][:], rows[0])
@@ -71,7 +70,7 @@ def tile_attend_pq_att_kernel(tc, qT, cb, norm, offs, offs2, out):
         nc.sync.dma_start(runs[1][:], rows[1, :, : RUN_ROWS[1], :])
         for (g, t), window in loaded_windows.items():
             nc.sync.dma_start(window[:], rows[g, :, t, :])
-        for g, m in ((0, 1), (1, 1), (0, 0), (1, 0)):
+        for g, m in ((0, 1), (1, 1), (0, 0)):
             nc.sync.dma_start(q_raw[g, m][:], q_rows[g][:, :, m_tiles[m]])
 
         nc.vector.tensor_copy(norm_spread[:], norm_part[:].unsqueeze(2).to_broadcast([P, NORM_RUN, BLOCK]))
@@ -93,7 +92,8 @@ def tile_attend_pq_att_kernel(tc, qT, cb, norm, offs, offs2, out):
         ]
         q_bf = {
             (g, m): keep.tile([P, M_TILE, ROWS], BF16, name=f"q_bf_{g}_{m}", align_bytes=MX_ALIGN)[:]
-            for g, m in q_raw
+            for g in range(PARTS)
+            for m in range(len(m_tiles))
         }
         q_codes = [keep.tile([P, NQ], U32, name=f"q_codes_{g}", align_bytes=MX_ALIGN) for g in range(PARTS)]
         q_scales = [keep.tile([P, NQ], U8, name=f"q_scales_{g}", align_bytes=MX_ALIGN) for g in range(PARTS)]
@@ -144,6 +144,9 @@ def tile_attend_pq_att_kernel(tc, qT, cb, norm, offs, offs2, out):
             if g == 0:
                 quantize(k_codes[g], k_scales[g], slice(0, N), k_bf[g][:])
 
+        q_raw[1, 0] = keep.tile([P, ROWS, M_TILE], F32, name=f"window_{RUN_ROWS[-1]}", align_bytes=DMA_ALIGN)
+        nc.sync.dma_start(q_raw[1, 0][:], q_rows[1][:, :, m_tiles[0]])
+
         weave(nc.scalar.copy, q_bf[0, 1], q_raw[0, 1][:])
         weave(nc.vector.tensor_copy, q_bf[1, 1], q_raw[1, 1][:])
         quantize_and_multiply(0, 1)
@@ -157,7 +160,7 @@ def tile_attend_pq_att_kernel(tc, qT, cb, norm, offs, offs2, out):
 
         results = [
             keep.tile([M_TILE, N], F32, name="result_0", align_bytes=DMA_ALIGN),
-            keep.tile([M_TILE, N], F32, name="q_raw_1_0", align_bytes=DMA_ALIGN),
+            keep.tile([M_TILE, N], F32, name="result_1", align_bytes=DMA_ALIGN),
         ]
         for bank, cols in zip(sums[1], halves):
             nc.scalar.copy(results[1][:, cols], bank[:])

@@ -84,40 +84,39 @@ def tile_attend_pq_att_kernel(tc, qT, cb, norm, offs, offs2, out):
             [keep.tile([P, ROWS, HALF], F32, name=f"k_f32_{g}_{h}") for h in range(len(halves))]
             for g in range(PARTS)
         ]
-        k_bf = [keep.tile([P, N, ROWS], BF16, name=f"k_bf_{g}", align_bytes=MX_ALIGN) for g in range(PARTS)]
-        k_codes = [keep.tile([P, N], U32, name=f"k_codes_{g}", align_bytes=MX_ALIGN) for g in range(PARTS)]
-        k_scales = [
-            keep.tile([P, N], U8, name="k_scales_0", align_bytes=MX_ALIGN),
-            keep.tile([P, N], U8, name="q_raw_1_1", align_bytes=DMA_ALIGN),
-        ]
-        q_bf = {
-            (g, m): keep.tile([P, M_TILE, ROWS], BF16, name=f"q_bf_{g}_{m}", align_bytes=MX_ALIGN)[:]
-            for g in range(PARTS)
-            for m in range(len(m_tiles))
-        }
-        q_codes = [keep.tile([P, NQ], U32, name=f"q_codes_{g}", align_bytes=MX_ALIGN) for g in range(PARTS)]
-        q_scales = [keep.tile([P, NQ], U8, name=f"q_scales_{g}", align_bytes=MX_ALIGN) for g in range(PARTS)]
+        def group(name, columns):
+            return (
+                keep.tile([P, columns, ROWS], BF16, name=f"{name}_bf", align_bytes=MX_ALIGN),
+                keep.tile([P, columns], U32, name=f"{name}_codes", align_bytes=MX_ALIGN),
+                keep.tile([P, columns], U8, name=f"{name}_scales", align_bytes=MX_ALIGN),
+            )
+
+        def columns_of(tiles, cols):
+            values, codes, scales = tiles
+            return values[:, cols, :], codes[:, cols], scales[:, cols]
+
+        joint = group("joint", N + M_TILE)
+        k = [columns_of(group("k_0", N), slice(0, N)), columns_of(joint, slice(0, N))]
+        k_bf = [values for values, codes, scales in k]
+        q = {(g, m): columns_of(group(f"q_{g}_{m}", M_TILE), slice(0, M_TILE)) for g, m in ((0, 0), (0, 1), (1, 0))}
+        q[1, 1] = columns_of(joint, slice(N, N + M_TILE))
+        q_bf = {piece: values for piece, (values, codes, scales) in q.items()}
         sums = [
             [psum.tile([M_TILE, HALF], F32, name=f"sums_{m}_{h}") for h in range(len(halves))]
             for m in range(len(m_tiles))
         ]
 
-        def quantize(codes, scales, cols, values):
-            nc.vector.quantize_mx(
-                out=codes[:, cols].bitcast(FP8X4),
-                scales=scales[:, cols],
-                in_=values.rearrange("p c t -> p (c t)"),
-            )
+        def quantize(values, codes, scales):
+            nc.vector.quantize_mx(out=codes.bitcast(FP8X4), scales=scales, in_=values.rearrange("p c t -> p (c t)"))
 
-        def quantize_and_multiply(g, m):
-            quantize(q_codes[g], q_scales[g], m_tiles[m], q_bf[g, m])
+        def multiply(g, m):
             for bank, cols in zip(sums[m], halves):
                 nc.tensor.matmul_mx(
                     out=bank[:],
-                    lhsT=q_codes[g][:, m_tiles[m]].bitcast(FP8X4),
-                    lhsT_scale=q_scales[g][:, m_tiles[m]],
-                    rhs=k_codes[g][:, cols].bitcast(FP8X4),
-                    rhs_scale=k_scales[g][:, cols],
+                    lhsT=q[g, m][1].bitcast(FP8X4),
+                    lhsT_scale=q[g, m][2],
+                    rhs=k[g][1][:, cols].bitcast(FP8X4),
+                    rhs_scale=k[g][2][:, cols],
                     start=(g == 0),
                     stop=(g == PARTS - 1),
                 )
@@ -142,21 +141,23 @@ def tile_attend_pq_att_kernel(tc, qT, cb, norm, offs, offs2, out):
             for h, cols in enumerate(halves):
                 nc.vector.tensor_copy(k_bf[g][:, cols, last], k_f32[g][h][:, last, :])
             if g == 0:
-                quantize(k_codes[g], k_scales[g], slice(0, N), k_bf[g][:])
+                quantize(*k[g])
 
         q_raw[1, 0] = keep.tile([P, ROWS, M_TILE], F32, name=f"window_{RUN_ROWS[-1]}", align_bytes=DMA_ALIGN)
         nc.sync.dma_start(q_raw[1, 0][:], q_rows[1][:, :, m_tiles[0]])
 
         weave(nc.scalar.copy, q_bf[0, 1], q_raw[0, 1][:])
         weave(nc.vector.tensor_copy, q_bf[1, 1], q_raw[1, 1][:])
-        quantize_and_multiply(0, 1)
-        quantize(k_codes[1], k_scales[1], slice(0, N), k_bf[1][:])
-        quantize_and_multiply(1, 1)
+        quantize(*q[0, 1])
+        multiply(0, 1)
+        quantize(*columns_of(joint, slice(0, N + M_TILE)))
+        multiply(1, 1)
         weave(nc.scalar.copy, q_bf[0, 0], q_raw[0, 0][:])
         for copy, queries in ((nc.vector.tensor_copy, slice(0, SHARE)), (nc.scalar.copy, slice(SHARE, M_TILE))):
             weave(copy, q_bf[1, 0][:, queries, :], q_raw[1, 0][:, :, queries])
-        quantize_and_multiply(0, 0)
-        quantize_and_multiply(1, 0)
+        for g in range(PARTS):
+            quantize(*q[g, 0])
+            multiply(g, 0)
 
         results = [
             keep.tile([M_TILE, N], F32, name="result_0", align_bytes=DMA_ALIGN),

@@ -101,16 +101,17 @@ def tile_attend_pq_att_kernel(tc, qT, cb, norm, offs, offs2, out):
         q = {(g, m): columns_of(group(f"q_{g}_{m}", M_TILE), slice(0, M_TILE)) for g, m in ((0, 0), (0, 1), (1, 0))}
         q[1, 1] = columns_of(joint, slice(N, N + M_TILE))
         q_bf = {piece: values for piece, (values, codes, scales) in q.items()}
+        bank_columns = [halves, [slice(0, N)]]
         sums = [
-            [psum.tile([M_TILE, HALF], F32, name=f"sums_{m}_{h}") for h in range(len(halves))]
-            for m in range(len(m_tiles))
+            [psum.tile([M_TILE, cols.stop - cols.start], F32, name=f"sums_{m}_{b}") for b, cols in enumerate(columns)]
+            for m, columns in enumerate(bank_columns)
         ]
 
         def quantize(values, codes, scales):
             nc.vector.quantize_mx(out=codes.bitcast(FP8X4), scales=scales, in_=values.rearrange("p c t -> p (c t)"))
 
         def multiply(g, m):
-            for bank, cols in zip(sums[m], halves):
+            for bank, cols in zip(sums[m], bank_columns[m]):
                 nc.tensor.matmul_mx(
                     out=bank[:],
                     lhsT=q[g, m][1].bitcast(FP8X4),
@@ -163,8 +164,7 @@ def tile_attend_pq_att_kernel(tc, qT, cb, norm, offs, offs2, out):
             keep.tile([M_TILE, N], F32, name="result_0", align_bytes=DMA_ALIGN),
             keep.tile([M_TILE, N], F32, name="result_1", align_bytes=DMA_ALIGN),
         ]
-        for bank, cols in zip(sums[1], halves):
-            nc.scalar.copy(results[1][:, cols], bank[:])
+        nc.scalar.copy(results[1][:], sums[1][0][:])
         nc.sync.dma_start(out[0, m_tiles[1], :], results[1][:])
         for copy, queue, bank, cols in zip(
             (nc.scalar.copy, nc.vector.tensor_copy), (nc.scalar, nc.sync), sums[0], halves

@@ -65,9 +65,9 @@ def tile_attend_pq_att_kernel(tc, qT, cb, norm, offs, offs2, out):
 
         nc.sync.dma_start(runs[0][:], rows[0])
         nc.sync.dma_start(offsets[:], offs)
-        nc.sync.dma_start(offsets2[:], offs2)
         nc.scalar.dma_start(norm_part[:], norm[0 : P // BLOCK, :].rearrange("r (i e) -> (r i) e", e=NORM_RUN))
         nc.sync.dma_start(runs[1][:], rows[1, :, : RUN_ROWS[1], :])
+        nc.sync.dma_start(offsets2[:], offs2)
         for (g, t), window in loaded_windows.items():
             nc.sync.dma_start(window[:], rows[g, :, t, :])
         for g, m in ((0, 1), (1, 1), (0, 0)):

@@ -24,7 +24,7 @@ NORM_RUN = N // BLOCK
 LINE = 4
 DMA_ALIGN = 256
 MX_ALIGN = 64
-SHARE = 80
+SHARE = 64
 RUN_ROWS = (4, 2)
 
 

@@ -136,13 +136,16 @@ def tile_attend_pq_att_kernel(tc, qT, cb, norm, offs, offs2, out):
                     nc.vector.tensor_tensor(
                         k_f32[g][h][:, t, :], window[:].indirect(entries), norm_row[:, cols], MULT
                     )
-                if t == last - 1:
+                if (g, t) == (PARTS - 1, last - 1):
                     for h, cols in enumerate(halves):
                         weave(nc.vector.tensor_copy, k_bf[g][:, cols, :last], k_f32[g][h][:, :last, :])
-            for h, cols in enumerate(halves):
-                nc.vector.tensor_copy(k_bf[g][:, cols, last], k_f32[g][h][:, last, :])
             if g == 0:
+                for h, cols in enumerate(halves):
+                    weave(nc.scalar.copy, k_bf[g][:, cols, :], k_f32[g][h][:])
                 quantize(*k[g])
+            else:
+                for h, cols in enumerate(halves):
+                    nc.vector.tensor_copy(k_bf[g][:, cols, last], k_f32[g][h][:, last, :])
 
         q_raw[1, 0] = keep.tile([P, ROWS, M_TILE], F32, name=f"window_{RUN_ROWS[-1]}", align_bytes=DMA_ALIGN)
         nc.sync.dma_start(q_raw[1, 0][:], q_rows[1][:, :, m_tiles[0]])

import concourse.mybir as mybir

FLOPS = 2 * 256 * 256 * 1024

F32 = mybir.dt.float32
BF16 = mybir.dt.bfloat16
U32 = mybir.dt.uint32
U16 = mybir.dt.uint16
U8 = mybir.dt.uint8
FP8X4 = mybir.dt.float8_e4m3fn_x4
MULT = mybir.AluOpType.mult

P = 128
PARTS = 2
ROWS = 4
CODEWORDS = 4096
NQ = 256
N = 256
HALF = 128
M_TILE = 128
LIST_GROUP = 16
BLOCK = 32
NORM_RUN = N // BLOCK
LINE = 4
DMA_ALIGN = 256
MX_ALIGN = 64
SHARE = 64
RUN_ROWS = (4, 2)


def weave(copy, dst, src):
    copy(dst.rearrange("p (c i) t -> p c t i", i=LINE), src.rearrange("p t (c i) -> p c t i", i=LINE))


def tile_attend_pq_att_kernel(tc, qT, cb, norm, offs, offs2, out):
    nc = tc.nc
    rows = cb.rearrange("(g p t) c -> g p t c", g=PARTS, p=P, t=ROWS)
    q_rows = qT[0].rearrange("(g p t) q -> g p t q", g=PARTS, t=ROWS)
    halves = [slice(h * HALF, (h + 1) * HALF) for h in range(N // HALF)]
    m_tiles = [slice(m * M_TILE, (m + 1) * M_TILE) for m in range(NQ // M_TILE)]

    with (
        tc.tile_pool(name="keep", bufs=1) as keep,
        tc.tile_pool(name="ring", bufs=2) as ring,
        tc.psum_pool(name="psum", bufs=1) as psum,
    ):
        offsets = keep.tile([P, N // LIST_GROUP], U16, name="offsets", align_bytes=DMA_ALIGN)
        offsets2 = keep.tile([P, N // LIST_GROUP], U16, name="offsets2", align_bytes=DMA_ALIGN)
        norm_part = keep.tile([P, NORM_RUN], F32, name="norm_part", align_bytes=DMA_ALIGN)
        norm_spread = keep.tile([P, NORM_RUN, BLOCK], F32, name="norm_spread", align_bytes=MX_ALIGN)
        norm_turned = keep.tile([P, N], F32, name="norm_turned", align_bytes=MX_ALIGN)
        norm_row = keep.tile([P, N], F32, name="norm_row")
        runs = [
            keep.tile([P, count, CODEWORDS], F32, name=f"run_{g}", align_bytes=DMA_ALIGN)
            for g, count in enumerate(RUN_ROWS)
        ]
        loaded_windows = {
            (PARTS - 1, t): keep.tile([P, CODEWORDS], F32, name=f"window_{t}", align_bytes=DMA_ALIGN)
            for t in range(RUN_ROWS[-1], ROWS)
        }
        q_raw = {
            (g, m): keep.tile([P, ROWS, M_TILE], F32, name=f"q_raw_{g}_{m}", align_bytes=DMA_ALIGN)
            for g, m in ((0, 0), (0, 1), (1, 1))
        }

        nc.sync.dma_start(runs[0][:], rows[0])
        nc.sync.dma_start(offsets[:], offs)
        nc.scalar.dma_start(norm_part[:], norm[0 : P // BLOCK, :].rearrange("r (i e) -> (r i) e", e=NORM_RUN))
        nc.sync.dma_start(runs[1][:], rows[1, :, : RUN_ROWS[1], :])
        nc.sync.dma_start(offsets2[:], offs2)
        for (g, t), window in loaded_windows.items():
            nc.sync.dma_start(window[:], rows[g, :, t, :])
        for g, m in ((0, 1), (1, 1), (0, 0)):
            nc.sync.dma_start(q_raw[g, m][:], q_rows[g][:, :, m_tiles[m]])

        nc.vector.tensor_copy(norm_spread[:], norm_part[:].unsqueeze(2).to_broadcast([P, NORM_RUN, BLOCK]))
        nc.vector.transpose(norm_turned[:], norm_spread[:].rearrange("p e j -> p (e j)"))
        nc.vector.tensor_copy(
            norm_row[:].rearrange("p (i e) -> p i e", e=NORM_RUN),
            norm_turned[:].rearrange("p (e i) -> p i e", e=NORM_RUN),
        )

        k_f32 = [
            [keep.tile([P, ROWS, HALF], F32, name=f"k_f32_{g}_{h}") for h in range(len(halves))]
            for g in range(PARTS)
        ]
        def group(name, columns):
            return (
                keep.tile([P, columns, ROWS], BF16, name=f"{name}_bf", align_bytes=MX_ALIGN),
                keep.tile([P, columns], U32, name=f"{name}_codes", align_bytes=MX_ALIGN),
                keep.tile([P, columns], U8, name=f"{name}_scales", align_bytes=MX_ALIGN),
            )

        def columns_of(tiles, cols):
            values, codes, scales = tiles
            return values[:, cols, :], codes[:, cols], scales[:, cols]

        joint = group("joint", N + M_TILE)
        k = [columns_of(group("k_0", N), slice(0, N)), columns_of(joint, slice(0, N))]
        k_bf = [values for values, codes, scales in k]
        q = {(g, m): columns_of(group(f"q_{g}_{m}", M_TILE), slice(0, M_TILE)) for g, m in ((0, 0), (0, 1), (1, 0))}
        q[1, 1] = columns_of(joint, slice(N, N + M_TILE))
        q_bf = {piece: values for piece, (values, codes, scales) in q.items()}
        bank_columns = [halves, [slice(0, N)]]
        sums = [
            [psum.tile([M_TILE, cols.stop - cols.start], F32, name=f"sums_{m}_{b}") for b, cols in enumerate(columns)]
            for m, columns in enumerate(bank_columns)
        ]

        def quantize(values, codes, scales):
            nc.vector.quantize_mx(out=codes.bitcast(FP8X4), scales=scales, in_=values.rearrange("p c t -> p (c t)"))

        def multiply(g, m):
            for bank, cols in zip(sums[m], bank_columns[m]):
                nc.tensor.matmul_mx(
                    out=bank[:],
                    lhsT=q[g, m][1].bitcast(FP8X4),
                    lhsT_scale=q[g, m][2],
                    rhs=k[g][1][:, cols].bitcast(FP8X4),
                    rhs_scale=k[g][2][:, cols],
                    start=(g == 0),
                    stop=(g == PARTS - 1),
                )

        last = ROWS - 1
        for g, lists in enumerate((offsets, offsets2)):
            for t in range(ROWS):
                if t < RUN_ROWS[g]:
                    by_scalar = t % 2 == 1
                    window = ring.tile([P, CODEWORDS], F32, name="by_scalar" if by_scalar else "by_vector")
                    (nc.scalar.copy if by_scalar else nc.vector.tensor_copy)(window[:], runs[g][:, t, :])
                else:
                    window = loaded_windows[g, t]
                for h, cols in enumerate(halves):
                    entries = lists[:, h * HALF // LIST_GROUP : (h + 1) * HALF // LIST_GROUP]
                    nc.vector.tensor_tensor(
                        k_f32[g][h][:, t, :], window[:].indirect(entries), norm_row[:, cols], MULT
                    )
                if (g, t) == (PARTS - 1, last - 1):
                    for h, cols in enumerate(halves):
                        weave(nc.vector.tensor_copy, k_bf[g][:, cols, :last], k_f32[g][h][:, :last, :])
            if g == 0:
                for h, cols in enumerate(halves):
                    weave(nc.scalar.copy, k_bf[g][:, cols, :], k_f32[g][h][:])
                quantize(*k[g])
            else:
                for h, cols in enumerate(halves):
                    nc.vector.tensor_copy(k_bf[g][:, cols, last], k_f32[g][h][:, last, :])

        q_raw[1, 0] = keep.tile([P, ROWS, M_TILE], F32, name=f"window_{RUN_ROWS[-1]}", align_bytes=DMA_ALIGN)
        nc.sync.dma_start(q_raw[1, 0][:], q_rows[1][:, :, m_tiles[0]])

        weave(nc.scalar.copy, q_bf[0, 1], q_raw[0, 1][:])
        weave(nc.vector.tensor_copy, q_bf[1, 1], q_raw[1, 1][:])
        quantize(*q[0, 1])
        multiply(0, 1)
        quantize(*columns_of(joint, slice(0, N + M_TILE)))
        multiply(1, 1)
        weave(nc.scalar.copy, q_bf[0, 0], q_raw[0, 0][:])
        for copy, queries in ((nc.vector.tensor_copy, slice(0, SHARE)), (nc.scalar.copy, slice(SHARE, M_TILE))):
            weave(copy, q_bf[1, 0][:, queries, :], q_raw[1, 0][:, :, queries])
        for g in range(PARTS):
            quantize(*q[g, 0])
            multiply(g, 0)

        results = [
            keep.tile([M_TILE, N], F32, name="result_0", align_bytes=DMA_ALIGN),
            keep.tile([M_TILE, N], F32, name="result_1", align_bytes=DMA_ALIGN),
        ]
        nc.scalar.copy(results[1][:], sums[1][0][:])
        nc.sync.dma_start(out[0, m_tiles[1], :], results[1][:])
        for copy, queue, bank, cols in zip(
            (nc.scalar.copy, nc.vector.tensor_copy), (nc.scalar, nc.sync), sums[0], halves
        ):
            copy(results[0][:, cols], bank[:])
            queue.dma_start(out[0, m_tiles[0], cols], results[0][:, cols])
